import numpy as np, ml_dtypes
CORES = [2,6,10,14,18,22,26,30]
N = 8
BF = ml_dtypes.bfloat16
def gentries(a):
    return np.ascontiguousarray(a.reshape(8, 16, -1).transpose(0, 2, 1)).reshape(8, -1)
def gtable(e):
    e = np.asarray(e); return np.ascontiguousarray(e.reshape(8, -1, 16).transpose(0, 2, 1)).reshape(128, -1).astype(np.int32)
V, S, G, OFF, DEP, Q = 3072, 3072, 128, (1, 2, 3, 4, 5, 6, 7), 4, 8
B = len(OFF); W = S + B * G
def parts(rng):
    h = rng.integers(0, 128, (N, 8, 16, V)); v = rng.integers(0, 128, (N, 8, 16, S))
    e = rng.integers(0, 16, (N, 8, V)); k0 = rng.integers(0, V, (N, 8, V)); k1 = rng.integers(0, V, (N, 8, V))
    p = rng.integers(0, W, (N, 8, 16, S)); n = rng.integers(0, V, (N, 8, S))
    b = np.ascontiguousarray(np.argsort(rng.random((N, 8, B, S)), axis=-1)[..., :G])
    return h, v, e, k0, k1, p, n, b
def pack(h, v, e, k0, k1, p, n, b):
    return {"hist": np.ascontiguousarray(h.reshape(N, 128, V)).astype(np.float32).astype(BF), "x": np.ascontiguousarray(v.reshape(N, 128, S)).astype(np.float32).astype(BF),
            "way": e.astype(np.int32), "kid0": k0.astype(np.int32), "kid1": k1.astype(np.int32), "nb": np.ascontiguousarray(p.reshape(N, 128, S)).astype(np.int32),
            "nd0": np.stack([gtable(a) for a in n]), "bd": np.stack([gtable(a.reshape(8, -1)) for a in b])}
def setup_inputs(rng):
    return pack(*parts(rng))
def setup_inputs_ties(rng):
    h, v, e, k0, k1, p, n, b = parts(rng)
    hb = rng.choice(np.array([0, 63, 126]), (1, 8, 16, 1)); xb = rng.choice(np.array([0, 64, 127]), (1, 8, 16, 1))
    hb[0, 0] = 126; xb[0, 0] = 127; hb[0, 1] = 0; xb[0, 1] = 0
    k = rng.choice(np.array([0, 0, 0, 0, Q - 1, Q, Q + 1, 16]), (N, 8, 1, V))
    place = np.argsort(rng.random((N, 8, 16, V)), axis=2)
    h = hb + (place < k); v = np.zeros((N, 8, 16, S), np.int64) + xb
    ends = np.array([0, 1, 126, 127])
    h[:, 6:] = rng.choice(ends, (N, 2, 16, V)); v[:, 6:] = rng.choice(ends, (N, 2, 16, S))
    return pack(h, v, e, k0, k1, p, n, b)
def setup_inputs_alike(rng):
    h, v, e, k0, k1, p, n, b = parts(rng)
    p[:, 1] = np.arange(S); p[:, 2] = rng.integers(S, W, (N, 16, S)); p[:, 3] = rng.integers(0, S, (N, 16, S))
    p[:, 4] = rng.choice(np.array([0, S - 1, S, S + G - 1, W - G, W - 1]), (N, 16, S)); p[:, 5] = rng.integers(0, W, (N, 1, 1)); p[:, 6] = p[:, 6, :1]
    b[:, ::2] = rng.choice(np.array([0, S - 1, S // 2, 3]), (N, 4, B, G))
    e[:, 2:4] = rng.integers(0, 16, (N, 2, 1))
    b[:, 0] = rng.integers(1, S, (N, B, 1)); b[:, 7] = np.argsort(rng.random((N, S)), axis=-1)[:, :B * G].reshape(N, B, G)
    n[:, ::7] = np.argsort(rng.random((N, 2, V)), axis=-1)[..., :S]
    return pack(h, v, e, k0, k1, p, n, b)
def setup_inputs_meet(rng):
    h, v, e, k0, k1, p, n, b = parts(rng)
    n[:, :4] = rng.choice(np.array([0, 1, V // 2, V - 1]), (N, 4, S)); n[:, 0] = 0; n[:, 7] = V - 1 - rng.integers(0, 32, (N, S))
    k1[:, 2] = k0[:, 2]; k0[:, 3] = np.arange(V); k1[:, 3] = np.arange(V); k0[:, 4] = np.arange(V)
    k0[:, 5] = rng.choice(np.array([0, V - 1]), (N, V)); k1[:, 5] = rng.choice(np.array([0, V - 1]), (N, V))
    e[:, 6] = rng.choice(np.array([0, 15]), (N, V))
    return pack(h, v, e, k0, k1, p, n, b)
def setup_inputs_far(rng):
    h, v, e, k0, k1, p, n, b = parts(rng); half = V // 2
    h = rng.integers(0, 97, (N, 8, 1, 1)) + rng.integers(0, 31, h.shape); v = rng.integers(0, 97, (N, 8, 1, 1)) + rng.integers(0, 31, v.shape)
    p = rng.integers(S, W, p.shape); b[..., 0] = 0; b[..., G - 1] = S - 1
    e[:, :4] = rng.integers(0, 16, (N, 4, 1)); p[:, :2] = rng.integers(S, S + G, (N, 2, 16, S))
    n[:, 0] = rng.integers(0, V, (N, 1)); v[:, 0] = rng.integers(0, 128, (N, 16, S))
    h[:, 0] = rng.integers(0, 32, (N, 16, V)); h[1::2, 0] += 96
    v[:, 1] = rng.integers(0, 32, (N, 16, S)); h[::2, 1] = rng.integers(64, 80, (N // 2, 16, V)); k0[::2, 1] = np.arange(V)
    h[1::2, 1] = rng.integers(0, 128, (N // 2, 16, V)); h[1::2, 1, :, :half] = rng.integers(0, 16, (N // 2, 16, half))
    n[1::2, 1] = rng.integers(0, half, (N // 2, S))
    k0[1::2, 1, :half] = rng.integers(half, V, (N // 2, half)); k1[1::2, 1, :half] = rng.integers(half, V, (N // 2, half))
    return pack(h, v, e, k0, k1, p, n, b)
def setup_inputs_spread(rng):
    h, v, e, k0, k1, p, n, b = parts(rng)
    h = np.minimum((np.exp2(7 * rng.random((N, 8, 1, V))) * rng.random(h.shape)).astype(np.int64), 127)
    v = np.minimum((np.exp2(7 * rng.random((N, 8, 1, S))) * rng.random(v.shape)).astype(np.int64), 127)
    n = np.minimum((V * rng.random(n.shape) ** 3).astype(np.int64), V - 1); k1 = np.minimum((V * rng.random(k1.shape) ** 2).astype(np.int64), V - 1)
    p = W - 1 - np.minimum((W * rng.random(p.shape) ** 2).astype(np.int64), W - 1)
    b[:, ::2] = np.argsort(rng.random((N, 4, B, S // 2)), axis=-1)[..., :G] + S // 2 * rng.integers(0, 2, (N, 4, B, 1))
    return pack(h, v, e, k0, k1, p, n, b)
def check_inputs(d):
    bad = []
    for k in ("hist", "x"):
        a = np.asarray(d[k]).astype(np.float32)
        if not np.all((a >= 0) & (a <= 127) & (a == np.floor(a))): bad.append("whole numbers from 0 to 127 in " + k)
    for k, hi in (("way", 15), ("kid0", V - 1), ("kid1", V - 1), ("nb", W - 1), ("nd0", V - 1), ("bd", S - 1)):
        if np.min(d[k]) < 0 or np.max(d[k]) > hi: bad.append("range of " + k)
    return bad
def reference(hist, x, way, kid0, kid1, nb, nd0, bd):
    h = hist.astype(np.float32).astype(np.int32).reshape(N, 8, 16, V); xv = x.astype(np.float32).astype(np.int32).reshape(N, 8, 16, S)
    part = nb.astype(np.int64).reshape(N, 8, 16, S)
    n = np.stack([gentries(a) for a in nd0]).astype(np.int64)
    bl = np.stack([gentries(a) for a in bd]).astype(np.int64).reshape(N, 8, B, G)
    for depth in range(DEP):
        hn = np.stack([np.take_along_axis(h[a], n[a][:, None, :], 2) for a in range(N)])
        new = []
        for a in range(N):
            hw, xw = [hn[a]], [xv[a]]
            for i, d in enumerate(OFF):
                q = (a - d) % N; ix = bl[q, :, i][:, None, :]
                hw.append(np.take_along_axis(hn[q], ix, 2)); xw.append(np.take_along_axis(xv[q], ix, 2))
            hw, xw = np.concatenate(hw, axis=2), np.concatenate(xw, axis=2)
            e = np.take_along_axis(way[a].astype(np.int64), n[a], 1)
            p = np.take_along_axis(part[a], e[:, None, :], 1)
            more = xv[a] + np.take_along_axis(hw, p, 2) > np.take_along_axis(xw, p, 2) + hn[a]
            right = np.add.reduce(more.astype(np.int32), axis=1) >= Q
            new.append(np.where(right, np.take_along_axis(kid1[a], n[a], 1), np.take_along_axis(kid0[a], n[a], 1)))
        n = np.stack(new).astype(np.int64)
    return {"y": n.astype(np.float32)}

@@ -1,0 +1,376 @@
+from concourse.bass import DstId, RemoteDMATransfer
+from concourse.mybir import AluOpType as ALU, ActivationFunctionType as ACT
+
+S = 3072
+G = 128
+NB = 7
+W = S + NB * G
+DEP = 4
+CH = 1024
+NC = CH // 16
+
+SCRATCH = {
+    "ps": ("psum", [128, 4096], "float32"),
+    "ones": ("sbuf", [128, 768], "bfloat16"),
+    "bc": ("sbuf", [128, 768], "bfloat16"),
+    "z": ("sbuf", [128, 144], "bfloat16"),
+    "zt": ("sbuf", [128, 8], "bfloat16"),
+    "pi": ("sbuf", [128, 8], "int32"),
+    "pe": ("sbuf", [128, 8], "int32"),
+    "ecol": ("sbuf", [128, 8], "float32"),
+    "nege": ("sbuf", [128, 8], "float32"),
+    "wayi": ("sbuf", [128, 512], "int32"),
+    "wayb": ("sbuf", [128, 512], "bfloat16"),
+    "kidi": ("sbuf", [128, 384], "int32"),
+    "ka": ("sbuf", [128, 192], "int32"),
+    "kb": ("sbuf", [128, 192], "int32"),
+    "kl": ("sbuf", [128, 192], "int32"),
+    "pcs": ("sbuf", [128, 768], "bfloat16"),
+    "ndi": ("sbuf", [128, 192], "int32"),
+    "bdi": ("sbuf", [128, 56], "int32"),
+    "bdl": ("sbuf", [128, 56], "uint16"),
+    "hs": ("sbuf", [128, S], "bfloat16"),
+    "xs": ("sbuf", [128, S], "bfloat16"),
+    "nbi": ("sbuf", [128, S], "int32"),
+    "nbh": ("sbuf", [128, S], "float16"),
+    "oh": ("sbuf", [128, S], "bfloat16"),
+    "kt": ("sbuf", [128, S], "bfloat16"),
+    "ab": ("sbuf", [128, CH], "bfloat16"),
+    "yf": ("sbuf", [128, 192], "float32"),
+}
+for _d in range(DEP):
+    SCRATCH["e%d" % _d] = ("sbuf", [128, W], "bfloat16")
+    SCRATCH["ec%d" % _d] = ("sbuf", [128, CH], "bfloat16")
+    SCRATCH["hn%d" % _d] = ("sbuf", [128, 2 * CH], "bfloat16")
+    SCRATCH["q%d" % _d] = ("sbuf", [128, S], "float16")
+    SCRATCH["kg%d" % _d] = ("sbuf", [128, S], "bfloat16")
+    SCRATCH["ep%d" % _d] = ("sbuf", [128, 2 * CH], "bfloat16")
+    SCRATCH["cm%d" % _d] = ("sbuf", [128, S], "bfloat16")
+    SCRATCH["sb%d" % _d] = ("sbuf", [128, NB * G], "bfloat16")
+    SCRATCH["sf%d" % _d] = ("sbuf", [128, 192], "float32")
+    SCRATCH["ti%d" % _d] = ("sbuf", [128, 192], "int32")
+    SCRATCH["ui%d" % _d] = ("sbuf", [128, 192], "int32")
+    SCRATCH["nl%d" % _d] = ("sbuf", [128, 192], "uint16")
+    SCRATCH["pl%d" % _d] = ("sbuf", [128, 192], "uint16")
+
+SEMAPHORES = ["snd"] + ["arr%d" % _d for _d in range(DEP)] + ["s%d" % _i for _i in range(120)]
+
+
+def bits(engs):
+    m = 0
+    for e in engs:
+        m |= 1 << e
+    return m
+
+
+def border_calls(q, cores, topo):
+    n = len(cores)
+    src = cores[q]
+    dst = [(q + b + 1) % n for b in range(NB)]
+    off = [b for b in range(NB) if topo.chip(cores[dst[b]]) != topo.chip(src)]
+    first = None
+    for a in (0, NB - 4):
+        if all(b in off for b in range(a, a + 4)):
+            first = list(range(a, a + 4))
+            break
+    rest = [b for b in range(NB) if b not in first]
+    oe = topo.engines(src, cores[dst[first[0]]])
+    k = len(oe) // 4
+    c1 = [(b, dst[b], oe[i * k:(i + 1) * k]) for i, b in enumerate(first)]
+    ro = [b for b in rest if b in off]
+    k = len(oe) // len(ro)
+    while k & (k - 1):
+        k -= 1
+    c2 = []
+    used = 0
+    for b in rest:
+        if b in off:
+            i = ro.index(b)
+            c2.append((b, dst[b], oe[i * k:(i + 1) * k]))
+        else:
+            free = [e for e in topo.engines(src, cores[dst[b]]) if e not in oe]
+            c2.append((b, dst[b], [free[used], free[used + 2]]))
+            used += 4
+    return [c1, c2]
+
+
+def rank_program(g, core, T, topo):
+    rank = T.rank_of(core)
+    if rank is None:
+        return
+    cores = list(T.cores)
+    n = len(cores)
+    Q = {"g": g, "v": g.vector, "s": g.scalar, "t": g.tensor, "y": g.sync}
+    V, A, P = g.vector, g.scalar, g.tensor
+    names = {}
+    count = {}
+    seen = {k: {} for k in Q}
+    top = {}
+
+    def need(e, deps):
+        for d in deps:
+            if d is None:
+                continue
+            nm, c = d
+            if seen[e].get(nm, 0) < c:
+                Q[e].wait_ge(T.sem[nm], c)
+                seen[e][nm] = c
+                top[nm] = max(top.get(nm, 0), c)
+
+    def op(e, role, deps, fn, inc=1):
+        need(e, deps)
+        if role not in names:
+            names[role] = "s%d" % len(names)
+        nm = names[role]
+        count[nm] = count.get(nm, 0) + inc
+        fn().then_inc(T.sem[nm], inc)
+        return (nm, count[nm])
+
+    def dma(e, role, deps, out, in_):
+        return op(e, role, deps, lambda: Q[e].dma_start(out, in_), 16)
+
+    def ts(role, deps, out, in0, s1, o0, s2=None, o1=None):
+        if o1 is None:
+            return op("v", role, deps, lambda: V.tensor_scalar(out, in0, s1, None, o0))
+        return op("v", role, deps, lambda: V.tensor_scalar(out, in0, s1, s2, o0, o1))
+
+    def tt(role, deps, out, a, b, o):
+        return op("v", role, deps, lambda: V.tensor_tensor(out, a, b, o))
+
+    def cp(role, deps, out, a):
+        return op("v", role, deps, lambda: V.tensor_copy(out, a))
+
+    def sg(role, deps, out, win, off):
+        return op("s", role, deps, lambda: A.activation(out, win.indirect(off), ACT.Copy))
+
+    def ch(t, j):
+        return t[:, CH * j:CH * (j + 1)]
+
+    def lc(t, j):
+        return t[:, NC * j:NC * (j + 1)]
+
+    def select(role, deps, out, src, j, rows):
+        need("t", deps)
+
+        def rhs(r):
+            if rows:
+                return src[:, CH * j + NC * r:CH * j + NC * (r + 1)]
+            return src[:, CH * j + r:CH * (j + 1):16]
+        for r in range(15):
+            P.matmul(out, T.z[:, 15 - r:143 - r], rhs(r), r == 0, False)
+        return op("t", role, [], lambda: P.matmul(out, T.z[:, 0:128], rhs(15), False, True))
+
+    ps = T.ps
+
+    def pbank(j):
+        return ps[:, 512 * j:512 * j + NC]
+
+    def kbank(j):
+        return ps[:, 512 * (3 + j):512 * (3 + j) + NC]
+
+    def cbank(j):
+        return ps[:, 512 * (3 + j) + NC:512 * (3 + j) + 2 * NC]
+
+    l_way = dma("y", "l_way", [], T.wayi[0:48, :], T.way[:])
+    l_k0 = dma("s", "l_k0", [], T.kidi[:, 0:192], T.kid0[:])
+    l_k1 = dma("s", "l_k1", [], T.kidi[:, 192:384], T.kid1[:])
+    l_nd = dma("y", "l_nd", [], T.ndi[:], T.nd0[:])
+    l_h = dma("y", "l_h", [], T.hs[:], T.hist[:])
+    l_bd = dma("s", "l_bd", [], T.bdi[:], T.bd[:])
+    l_x = {}
+    for j in (2, 0, 1):
+        l_x[j] = dma("y", "l_x%d" % j, [], ch(T.xs, j), ch(T.x, j))
+    l_nb = {0: dma("y", "l_nb0", [], ch(T.nbi, 0), ch(T.nb, 0))}
+
+    t_pi = op("g", "pi", [], lambda: g.iota(T.pi[:, 0:1], [[0, 1]], 0, 1))
+    t_one = op("v", "one", [], lambda: V.memset(T.ones[:], 1.0))
+    t_z0 = op("v", "z0", [], lambda: V.memset(T.z[:], 0.0))
+    t_bc = op("g", "bc", [t_one], lambda: g.affine_select(
+        T.bc[0:48, :], T.ones[0:48, :], [[-1, 6], [-6, 8], [0, 16]], ALU.is_equal, 0.0, 0, 1))
+    t_zt = op("g", "zt", [], lambda: g.affine_select(T.zt[:], T.ones[:, 0:8], [[-16, 8]], ALU.is_ge, 0.0, 0, 1))
+    t_z = op("g", "z", [t_zt, t_z0], lambda: g.affine_select(
+        T.z[:, 15:143:16], T.zt[:], [[16, 8]], ALU.is_ge, 0.0, 15, -1))
+    t_pe = ts("pe", [t_pi], T.pe[:, 0:1], T.pi[:, 0:1], 15, ALU.bitwise_and)
+    t_k0 = op("v", "kz", [], lambda: V.memset(T.kt[:], 0.0))
+    t_ec = cp("ec", [t_pe], T.ecol[:, 0:1], T.pe[:, 0:1])
+    t_ne = ts("ne", [t_pe], T.nege[:, 0:1], T.pe[:, 0:1], -1.0, ALU.mult)
+
+    t_wb = cp("wb", [l_way], T.wayb[0:48, :], T.wayi[0:48, :])
+    mm = {}
+    for t in (4, 5, 0, 1, 2, 3):
+        mm[t] = op("t", "wm%d" % t, [t_wb, t_bc], lambda: P.matmul(
+            ps[:, 512 * t:512 * (t + 1)], T.bc[0:48, 128 * t:128 * (t + 1)], T.wayb[0:48, :], True, True))
+    t_ab = op("s", "ab", [mm[4], mm[5], t_ne], lambda: A.activation(
+        T.ab[:], ch(ps, 2), ACT.Abs, bias=T.nege[:, 0:1]))
+    t_oh2 = op("s", "oh2", [t_ab], lambda: A.activation(ch(T.oh, 2), T.ab[:], ACT.Relu, bias=1.0, scale=-1.0))
+
+    k0, k1 = T.kidi[:, 0:192], T.kidi[:, 192:384]
+
+    def pc(i):
+        return T.pcs[:, 192 * i:192 * (i + 1)]
+    t_p1 = ts("p1", [l_k0], pc(1), k0, -8.0, ALU.add, 0.0, ALU.max)
+    t_ka = ts("ka", [l_k1], T.ka[:], k1, 2048.0, ALU.add)
+    t_kl = ts("kl", [l_k1], T.kl[:], k1, 63, ALU.bitwise_and)
+    t_p0 = tt("p0", [t_p1], pc(0), k0, pc(1), ALU.subtract)
+    t_kb = ts("kb", [t_ka], T.kb[:], T.ka[:], 6, ALU.logical_shift_right, 63, ALU.bitwise_and)
+    t_p2 = ts("p2", [t_kl], pc(2), T.kl[:], 8192.0, ALU.mult)
+    t_nl = cp("nl", [l_nd], T.nl0[:], T.ndi[:])
+    t_p3 = ts("p3", [t_kb], pc(3), T.kb[:], -32.0, ALU.add, 524288.0, ALU.mult)
+    t_kt = []
+    for i, tk in enumerate((t_p0, t_p1, t_p2, t_p3)):
+        t_kt.append(dma("y", "kt%d" % i, [tk, t_k0], T.kt[i::16, :], pc(i)))
+    for j in (1, 2):
+        l_nb[j] = dma("y", "l_nb%d" % j, [], ch(T.nbi, j), ch(T.nb, j))
+    t_oh = []
+    for j in (0, 1):
+        t_oh.append(ts("oh%d" % j, [mm[2 * j], mm[2 * j + 1], t_ec], ch(T.oh, j), ch(ps, j),
+                       T.ecol[:, 0:1], ALU.is_equal))
+    t_oh.append(t_oh2)
+    t_bl = cp("bl", [l_bd], T.bdl[:], T.bdi[:])
+
+    calls = border_calls(rank, cores, topo)
+    arrive = 0
+    for q in range(n):
+        for c in border_calls(q, cores, topo):
+            for b, dst, engs in c:
+                if dst == rank:
+                    arrive += len(engs)
+    sent = [0]
+
+    def B(name, d):
+        return T["%s%d" % (name, d)]
+
+    pfree = {0: [t_oh[0]], 1: [t_oh[0]], 2: [t_oh[1]]}
+    kfree = {0: [t_oh[1]], 1: [t_ab], 2: [t_ab]}
+    st = {}
+
+    def g1_gather(d, j):
+        st["hn", j] = sg("hn%d" % j, [st["nl", j], l_h], ch(B("hn", d), j), T.hs[:], lc(B("nl", d), j))
+
+    def g1_sub(d, j):
+        st["e", j] = tt("e%d" % j, [st["hn", j], l_x[j]], ch(B("e", d), j), ch(B("hn", d), j), ch(T.xs, j), ALU.subtract)
+        if j == 0 and d > 0:
+            st["ec"] = dma("y", "ecp", [st["e", 0]], B("ec", d)[:], ch(B("e", d), 0))
+        if j == 1 and d == 0:
+            st["ec"] = cp("ecv", [st["e", 0]], B("ec", d)[:], ch(B("e", d), 0))
+
+    def g1_direct(d, j):
+        st["e", j] = tt("e%d" % j, [st["nl", j], l_h, l_x[j]], ch(B("e", d), j),
+                        T.hs[:].indirect(lc(B("nl", d), j)), ch(T.xs, j), ALU.subtract)
+
+    def border(d, i):
+        c = calls[i]
+        b0, b1 = c[0][0], c[-1][0] + 1
+        tk = sg("bg%d" % i, [st["e", 0], st["e", 1], st["e", 2], t_bl], B("sb", d)[:, G * b0:G * b1],
+                B("e", d)[:, 0:S], T.bdl[:, 8 * b0:8 * b1])
+        need("g", [tk])
+        trs = []
+        for b, dst, engs in c:
+            rid, pid, _se = topo.addr(cores[dst])
+            trs.append(RemoteDMATransfer(
+                dst_ids=[DstId(rid=rid, pnc=pid)], dma_engine_mask=bits(engs), remote_sem=T.sem["arr%d" % d],
+                src=B("sb", d)[:, G * b:G * (b + 1)], dst=B("e", d)[:, S + G * b:S + G * (b + 1)]))
+            sent[0] += len(engs)
+        g.remote_dma_fused(trs, local_sem=T.sem.snd)
+
+    def kid_gather(d, j):
+        st["kg", j] = sg("kg%d" % j, [st["nl", j]] + t_kt, ch(B("kg", d), j), T.kt[:], lc(B("nl", d), j))
+
+    def kid_sum(d, j):
+        st["k", j] = select("k%d" % j, [st["kg", j], t_z] + kfree[j], kbank(j), B("kg", d), j, d == DEP - 1)
+
+    def way_pick(d, j):
+        if d == 0:
+            st["nbh", j] = ts("nbh%d" % j, [l_nb[j]], ch(T.nbh, j), ch(T.nbi, j), -2048.0, ALU.add)
+        st["q", j] = tt("q%d" % j, [st["nl", j], st["nbh", j]] + t_oh, ch(B("q", d), j),
+                        T.oh[:].indirect(lc(B("nl", d), j)), ch(T.nbh, j), ALU.mult)
+
+    def p_sum(d, j):
+        st["p", j] = select("ps%d" % j, [st["q", j], t_z] + pfree[j], pbank(j), B("q", d), j, False)
+
+    def p_list(d, j):
+        st["pl", j] = ts("pl%d" % j, [st["p", j]], lc(B("pl", d), j), pbank(j), 2048.0, ALU.add)
+        pfree[j] = [st["pl", j]]
+
+    def arr(d):
+        return ("arr%d" % d, arrive)
+
+    def g3_direct(d, j):
+        st["cm", j] = tt("cm%d" % j, [st["pl", j], st["e", 0], st["e", 1], st["e", 2], st["ec"], arr(d)],
+                         ch(B("cm", d), j), B("e", d)[:].indirect(lc(B("pl", d), j)), B("ec", d)[:], ALU.is_gt)
+
+    def g3_gather(d, j):
+        st["ep", j] = sg("ep%d" % j, [st["pl", j], arr(d)], ch(B("ep", d), j - 1), B("e", d)[:], lc(B("pl", d), j))
+
+    def g3_cmp(d, j):
+        st["cm", j] = tt("cm%d" % j, [st["ep", j]], ch(B("cm", d), j), ch(B("ep", d), j - 1), ch(B("e", d), j), ALU.is_gt)
+
+    def c_sum(d, j):
+        st["c", j] = select("c%d" % j, [st["cm", j]], cbank(j), B("cm", d), j, d == DEP - 1)
+
+    def step(d, j):
+        a = ts("sa%d" % j, [st["c", j], st["k", j]], lc(B("sf", d), j), cbank(j), 7.5, ALU.is_lt, 2.0 ** -13, ALU.max)
+        b = tt("sb%d" % j, [a], lc(B("ti", d), j), lc(B("sf", d), j), kbank(j), ALU.mult)
+        kfree[j] = [b]
+        c = ts("sc%d" % j, [b], lc(B("ui", d), j), lc(B("ti", d), j), 4095, ALU.bitwise_and)
+        if d < DEP - 1:
+            st["nl", j] = cp("sd%d" % j, [c], lc(B("nl", d + 1), j), lc(B("ui", d), j))
+        else:
+            f = cp("sd%d" % j, [c], lc(T.yf, j), lc(B("ui", d), j))
+            st["y", j] = dma("y", "y%d" % j, [f], ch(T.y, j), lc(T.yf, j))
+
+    def middle(d):
+        border(d, 0)
+        border(d, 1)
+        if d == 0:
+            kid_gather(d, 0)
+        way_pick(d, 0)
+        kid_gather(d, 1)
+        kid_sum(d, 0)
+        p_sum(d, 0)
+        way_pick(d, 1)
+        p_list(d, 0)
+        kid_gather(d, 2)
+        p_sum(d, 1)
+        kid_sum(d, 1)
+        way_pick(d, 2)
+        p_list(d, 1)
+        p_sum(d, 2)
+
+    for j in range(3):
+        st["nl", j] = t_nl
+    g1_gather(0, 0)
+    g1_direct(0, 2)
+    g1_gather(0, 1)
+    g1_sub(0, 0)
+    g1_sub(0, 1)
+    middle(0)
+    for d in range(DEP):
+        more = d < DEP - 1
+        g3_direct(d, 0)
+        g3_gather(d, 1)
+        p_list(d, 2)
+        g3_gather(d, 2)
+        g3_cmp(d, 1)
+        c_sum(d, 0)
+        kid_sum(d, 2)
+        step(d, 0)
+        c_sum(d, 1)
+        g3_cmp(d, 2)
+        if more:
+            g1_gather(d + 1, 0)
+        step(d, 1)
+        c_sum(d, 2)
+        if more:
+            g1_gather(d + 1, 1)
+            g1_sub(d + 1, 0)
+        step(d, 2)
+        if more:
+            kid_gather(d + 1, 0)
+            g1_direct(d + 1, 2)
+            g1_sub(d + 1, 1)
+            middle(d + 1)
+
+    g.wait_ge(T.sem.snd, sent[0])
+    need("y", [st["y", j] for j in range(3)])
+    need("y", [(nm, c) for nm, c in count.items() if top.get(nm, 0) < c])

@@ -4,10 +4,15 @@ from concourse.mybir import AluOpType as ALU, ActivationFunctionType as ACT
 S = 3072
 G = 128
 NB = 7
-W = S + NB * G
+BS = NB * G
+BC = BS // 16
+W = S + BS
 DEP = 4
 CH = 1024
 NC = CH // 16
+HF = 512
+KC = (0, 1024, 2048, S)
+PC = (0, 1024, 2048, S)
 
 SCRATCH = {
     "ps": ("psum", [128, 4096], "float32"),
@@ -27,33 +32,34 @@ SCRATCH = {
     "kl": ("sbuf", [128, 192], "int32"),
     "pcs": ("sbuf", [128, 768], "bfloat16"),
     "ndi": ("sbuf", [128, 192], "int32"),
-    "bdi": ("sbuf", [128, 56], "int32"),
-    "bdl": ("sbuf", [128, 56], "uint16"),
+    "bdi": ("sbuf", [128, BC], "int32"),
+    "bdl": ("sbuf", [128, BC], "uint16"),
     "hs": ("sbuf", [128, S], "bfloat16"),
     "xs": ("sbuf", [128, S], "bfloat16"),
     "nbi": ("sbuf", [128, S], "int32"),
     "nbh": ("sbuf", [128, S], "float16"),
     "oh": ("sbuf", [128, S], "bfloat16"),
     "kt": ("sbuf", [128, S], "bfloat16"),
-    "ab": ("sbuf", [128, CH], "bfloat16"),
+    "ab": ("sbuf", [128, S], "bfloat16"),
+    "hn": ("sbuf", [128, S], "bfloat16"),
+    "ep": ("sbuf", [128, S], "bfloat16"),
+    "tq": ("sbuf", [128, S], "bfloat16"),
     "yf": ("sbuf", [128, 192], "float32"),
 }
 for _d in range(DEP):
     SCRATCH["e%d" % _d] = ("sbuf", [128, W], "bfloat16")
-    SCRATCH["ec%d" % _d] = ("sbuf", [128, CH], "bfloat16")
-    SCRATCH["hn%d" % _d] = ("sbuf", [128, 2 * CH], "bfloat16")
+    SCRATCH["ec%d" % _d] = ("sbuf", [128, 2 * CH], "bfloat16")
     SCRATCH["q%d" % _d] = ("sbuf", [128, S], "float16")
     SCRATCH["kg%d" % _d] = ("sbuf", [128, S], "bfloat16")
-    SCRATCH["ep%d" % _d] = ("sbuf", [128, 2 * CH], "bfloat16")
     SCRATCH["cm%d" % _d] = ("sbuf", [128, S], "bfloat16")
-    SCRATCH["sb%d" % _d] = ("sbuf", [128, NB * G], "bfloat16")
+    SCRATCH["sb%d" % _d] = ("sbuf", [128, BS], "bfloat16")
     SCRATCH["sf%d" % _d] = ("sbuf", [128, 192], "float32")
     SCRATCH["ti%d" % _d] = ("sbuf", [128, 192], "int32")
     SCRATCH["ui%d" % _d] = ("sbuf", [128, 192], "int32")
     SCRATCH["nl%d" % _d] = ("sbuf", [128, 192], "uint16")
     SCRATCH["pl%d" % _d] = ("sbuf", [128, 192], "uint16")
 
-SEMAPHORES = ["snd"] + ["arr%d" % _d for _d in range(DEP)] + ["s%d" % _i for _i in range(120)]
+SEMAPHORES = ["snd"] + ["arr%d" % _d for _d in range(DEP)] + ["s%d" % _i for _i in range(140)]
 
 
 def bits(engs):
@@ -68,119 +74,154 @@ def border_calls(q, cores, topo):
     src = cores[q]
     dst = [(q + b + 1) % n for b in range(NB)]
     off = [b for b in range(NB) if topo.chip(cores[dst[b]]) != topo.chip(src)]
-    first = None
-    for a in (0, NB - 4):
-        if all(b in off for b in range(a, a + 4)):
-            first = list(range(a, a + 4))
-            break
-    rest = [b for b in range(NB) if b not in first]
-    oe = topo.engines(src, cores[dst[first[0]]])
-    k = len(oe) // 4
-    c1 = [(b, dst[b], oe[i * k:(i + 1) * k]) for i, b in enumerate(first)]
-    ro = [b for b in rest if b in off]
-    k = len(oe) // len(ro)
-    while k & (k - 1):
-        k -= 1
-    c2 = []
-    used = 0
-    for b in rest:
-        if b in off:
-            i = ro.index(b)
-            c2.append((b, dst[b], oe[i * k:(i + 1) * k]))
-        else:
-            free = [e for e in topo.engines(src, cores[dst[b]]) if e not in oe]
-            c2.append((b, dst[b], [free[used], free[used + 2]]))
-            used += 4
-    return [c1, c2]
+    oe = topo.engines(src, cores[dst[off[0]]])
+    here = topo.chip(src)
+    plane = [b for b in off if topo.same_plane(here, topo.chip(cores[dst[b]]))]
+    mate = [b for b in off if topo.mates(here, topo.chip(cores[dst[b]]))]
+    far = [b for b in off if b not in plane and b not in mate]
+    helpers = [c for c in topo.cores_of(src) if c not in cores and topo.die(c) == topo.die(src)]
+    free = [e for e in topo.engines(src, helpers[0]) if e not in oe]
+    out = []
+    for mine, engs in ((plane, oe + free), (far, oe), (mate, oe)):
+        w = len(engs) // len(mine)
+        out.append([(b, dst[b], engs[i * w:(i + 1) * w], helpers[i] if mine is plane else None) for i, b in enumerate(mine)])
+    for b in range(NB):
+        if b not in off:
+            near = [c for c in out[1:] if c[0][0] == b + 1 or c[-1][0] == b - 1][0]
+            near.append((b, dst[b], free[0::2], None))
+            near.sort()
+    return out
+
+
+def hand_on(g, core, T, topo):
+    cores = list(T.cores)
+    for q in range(len(cores)):
+        for b, dst, engs, via in border_calls(q, cores, topo)[0]:
+            if via == core:
+                rid, pid, _se = topo.addr(cores[dst])
+                mine = topo.engines(core, cores[dst])
+                for d in range(DEP):
+                    g.wait_ge(T.sem["arr%d" % d], len(engs))
+                    g.remote_dma(T["e%d" % d][:, S + G * b:S + G * (b + 1)], T["sb%d" % d][:, 0:G], T.sem["arr%d" % d],
+                                 T.sem.snd, pid, rid, bits(mine))
+                g.wait_ge(T.sem.snd, DEP * len(mine))
 
 
 def rank_program(g, core, T, topo):
     rank = T.rank_of(core)
     if rank is None:
+        hand_on(g, core, T, topo)
         return
     cores = list(T.cores)
-    n = len(cores)
     Q = {"g": g, "v": g.vector, "s": g.scalar, "t": g.tensor, "y": g.sync}
     V, A, P = g.vector, g.scalar, g.tensor
     names = {}
     count = {}
     seen = {k: {} for k in Q}
     top = {}
+    before = {}
+    bank_use = {b: {} for b in range(8)}
+    made = {}
 
     def need(e, deps):
-        for d in deps:
-            if d is None:
-                continue
+        for d in reversed(deps):
             nm, c = d
             if seen[e].get(nm, 0) < c:
                 Q[e].wait_ge(T.sem[nm], c)
                 seen[e][nm] = c
                 top[nm] = max(top.get(nm, 0), c)
+                for k, v in before.get(d, {}).items():
+                    seen[e][k] = max(seen[e].get(k, 0), v)
 
-    def op(e, role, deps, fn, inc=1):
+    def need_banks(e, banks):
+        for b in banks:
+            need(e, [tk for q, tk in bank_use[b].items() if q != e])
+
+    def op(e, role, deps, fn, inc=1, banks=()):
         need(e, deps)
+        need_banks(e, banks)
         if role not in names:
             names[role] = "s%d" % len(names)
         nm = names[role]
         count[nm] = count.get(nm, 0) + inc
         fn().then_inc(T.sem[nm], inc)
+        before[nm, count[nm]] = dict(seen[e])
+        for b in banks:
+            bank_use[b][e] = (nm, count[nm])
         return (nm, count[nm])
 
     def dma(e, role, deps, out, in_):
         return op(e, role, deps, lambda: Q[e].dma_start(out, in_), 16)
 
-    def ts(role, deps, out, in0, s1, o0, s2=None, o1=None):
+    def ts(role, deps, out, in0, s1, o0, s2=None, o1=None, banks=()):
         if o1 is None:
-            return op("v", role, deps, lambda: V.tensor_scalar(out, in0, s1, None, o0))
-        return op("v", role, deps, lambda: V.tensor_scalar(out, in0, s1, s2, o0, o1))
+            return op("v", role, deps, lambda: V.tensor_scalar(out, in0, s1, None, o0), 1, banks)
+        return op("v", role, deps, lambda: V.tensor_scalar(out, in0, s1, s2, o0, o1), 1, banks)
 
-    def tt(role, deps, out, a, b, o):
-        return op("v", role, deps, lambda: V.tensor_tensor(out, a, b, o))
+    def tt(role, deps, out, a, b, o, banks=()):
+        return op("v", role, deps, lambda: V.tensor_tensor(out, a, b, o), 1, banks)
 
     def cp(role, deps, out, a):
         return op("v", role, deps, lambda: V.tensor_copy(out, a))
 
+    def act(role, deps, out, a, func, banks=(), **kw):
+        return op("s", role, deps, lambda: A.activation(out, a, func, **kw), 1, banks)
+
     def sg(role, deps, out, win, off):
-        return op("s", role, deps, lambda: A.activation(out, win.indirect(off), ACT.Copy))
+        return act(role, deps, out, win.indirect(off), ACT.Copy)
 
-    def ch(t, j):
-        return t[:, CH * j:CH * (j + 1)]
+    def mark(name, d, a, b, tk):
+        made.setdefault((name, d), []).append((a, b, tk))
 
-    def lc(t, j):
-        return t[:, NC * j:NC * (j + 1)]
+    def done(name, d, a, b):
+        got = [m for m in made[name, d] if m[0] < b and a < m[1]]
+        assert sum(min(m[1], b) - max(m[0], a) for m in got) == b - a
+        return [m[2] for m in got]
 
-    def select(role, deps, out, src, j, rows):
-        need("t", deps)
+    def cols(t, a, b):
+        return t[:, a:b]
 
-        def rhs(r):
-            if rows:
-                return src[:, CH * j + NC * r:CH * j + NC * (r + 1)]
-            return src[:, CH * j + r:CH * (j + 1):16]
-        for r in range(15):
-            P.matmul(out, T.z[:, 15 - r:143 - r], rhs(r), r == 0, False)
-        return op("t", role, [], lambda: P.matmul(out, T.z[:, 0:128], rhs(15), False, True))
+    def lst(t, a, b):
+        return t[:, a // 16:b // 16]
 
     ps = T.ps
 
-    def pbank(j):
-        return ps[:, 512 * j:512 * j + NC]
+    def bank_cols(bank, k):
+        return ps[:, HF * bank:HF * bank + k]
 
-    def kbank(j):
-        return ps[:, 512 * (3 + j):512 * (3 + j) + NC]
+    def sums(kind, a, b):
+        if kind == "partner":
+            c = 6 * HF + (a - PC[2]) // 16
+        else:
+            c = {"kid": HF, "count": 3 * HF}[kind] + (a - KC[1]) // 16
+        e = c + (b - a) // 16
+        return ps[:, c:e], list(range(c // HF, (e - 1) // HF + 1))
 
-    def cbank(j):
-        return ps[:, 512 * (3 + j) + NC:512 * (3 + j) + 2 * NC]
+    def select(role, deps, kind, src, a, b, rows=False):
+        z = T.z
+        out, banks = sums(kind, a, b)
+        need("t", deps)
+        need_banks("t", banks)
 
-    l_way = dma("y", "l_way", [], T.wayi[0:48, :], T.way[:])
-    l_k0 = dma("s", "l_k0", [], T.kidi[:, 0:192], T.kid0[:])
-    l_k1 = dma("s", "l_k1", [], T.kidi[:, 192:384], T.kid1[:])
-    l_nd = dma("y", "l_nd", [], T.ndi[:], T.nd0[:])
-    l_h = dma("y", "l_h", [], T.hs[:], T.hist[:])
-    l_bd = dma("s", "l_bd", [], T.bdi[:], T.bd[:])
-    l_x = {}
-    for j in (2, 0, 1):
-        l_x[j] = dma("y", "l_x%d" % j, [], ch(T.xs, j), ch(T.x, j))
-    l_nb = {0: dma("y", "l_nb0", [], ch(T.nbi, 0), ch(T.nb, 0))}
+        def rhs(r):
+            if rows:
+                k = (b - a) // 16
+                return src[:, a + k * r:a + k * (r + 1)]
+            return src[:, a + r:b:16]
+        for r in range(15):
+            P.matmul(out, z[:, 15 - r:143 - r], rhs(r), r == 0, False)
+        return op("t", role, [], lambda: P.matmul(out, z[:, 0:128], rhs(15), False, True), 1, banks)
+
+    def load(name, out, in_, j):
+        a, b = CH * j, CH * (j + 1)
+        mark(name, 0, a, b, dma("y", "l_%s%d" % (name, j), [], cols(out, a, b), cols(in_, a, b)))
+
+    whole = {"way": (T.wayi[0:48, :], T.way[:]), "kid0": (T.kidi[:, 0:192], T.kid0[:]), "kid1": (T.kidi[:, 192:384], T.kid1[:]),
+             "nd0": (T.ndi[:], T.nd0[:]), "hist": (T.hs[:], T.hist[:]), "bd": (T.bdi[:], T.bd[:])}
+    got = {}
+
+    def fetch(name):
+        got[name] = dma("s" if name in ("kid0", "kid1", "bd") else "y", "l_" + name, [], *whole[name])
 
     t_pi = op("g", "pi", [], lambda: g.iota(T.pi[:, 0:1], [[0, 1]], 0, 1))
     t_one = op("v", "one", [], lambda: V.memset(T.ones[:], 1.0))
@@ -195,182 +236,294 @@ def rank_program(g, core, T, topo):
     t_ec = cp("ec", [t_pe], T.ecol[:, 0:1], T.pe[:, 0:1])
     t_ne = ts("ne", [t_pe], T.nege[:, 0:1], T.pe[:, 0:1], -1.0, ALU.mult)
 
-    t_wb = cp("wb", [l_way], T.wayb[0:48, :], T.wayi[0:48, :])
-    mm = {}
-    for t in (4, 5, 0, 1, 2, 3):
-        mm[t] = op("t", "wm%d" % t, [t_wb, t_bc], lambda: P.matmul(
-            ps[:, 512 * t:512 * (t + 1)], T.bc[0:48, 128 * t:128 * (t + 1)], T.wayb[0:48, :], True, True))
-    t_ab = op("s", "ab", [mm[4], mm[5], t_ne], lambda: A.activation(
-        T.ab[:], ch(ps, 2), ACT.Abs, bias=T.nege[:, 0:1]))
-    t_oh2 = op("s", "oh2", [t_ab], lambda: A.activation(ch(T.oh, 2), T.ab[:], ACT.Relu, bias=1.0, scale=-1.0))
+    wbank = {4: 2, 5: 3, 0: 6, 1: 7, 2: 4, 3: 5}
 
-    k0, k1 = T.kidi[:, 0:192], T.kidi[:, 192:384]
+    def way_spread():
+        t_wb = cp("wb", [got["way"]], T.wayb[0:48, :], T.wayi[0:48, :])
+        for t, b in wbank.items():
+            got["spread"] = op("t", "wm%d" % t, [t_wb, t_bc], lambda: P.matmul(
+                bank_cols(b, HF), T.bc[0:48, 128 * t:128 * (t + 1)], T.wayb[0:48, :], True, True), 1, [b])
 
-    def pc(i):
-        return T.pcs[:, 192 * i:192 * (i + 1)]
-    t_p1 = ts("p1", [l_k0], pc(1), k0, -8.0, ALU.add, 0.0, ALU.max)
-    t_ka = ts("ka", [l_k1], T.ka[:], k1, 2048.0, ALU.add)
-    t_kl = ts("kl", [l_k1], T.kl[:], k1, 63, ALU.bitwise_and)
-    t_p0 = tt("p0", [t_p1], pc(0), k0, pc(1), ALU.subtract)
-    t_kb = ts("kb", [t_ka], T.kb[:], T.ka[:], 6, ALU.logical_shift_right, 63, ALU.bitwise_and)
-    t_p2 = ts("p2", [t_kl], pc(2), T.kl[:], 8192.0, ALU.mult)
-    t_nl = cp("nl", [l_nd], T.nl0[:], T.ndi[:])
-    t_p3 = ts("p3", [t_kb], pc(3), T.kb[:], -32.0, ALU.add, 524288.0, ALU.mult)
-    t_kt = []
-    for i, tk in enumerate((t_p0, t_p1, t_p2, t_p3)):
-        t_kt.append(dma("y", "kt%d" % i, [tk, t_k0], T.kt[i::16, :], pc(i)))
-    for j in (1, 2):
-        l_nb[j] = dma("y", "l_nb%d" % j, [], ch(T.nbi, j), ch(T.nb, j))
-    t_oh = []
-    for j in (0, 1):
-        t_oh.append(ts("oh%d" % j, [mm[2 * j], mm[2 * j + 1], t_ec], ch(T.oh, j), ch(ps, j),
-                       T.ecol[:, 0:1], ALU.is_equal))
-    t_oh.append(t_oh2)
-    t_bl = cp("bl", [l_bd], T.bdl[:], T.bdi[:])
+    def way_onehot(j, e):
+        assert got["spread"]
+        a, b, k = CH * j, CH * (j + 1), wbank[2 * j]
+        if e == "v":
+            tk = ts("oh%d" % j, [t_ec], cols(T.oh, a, b), bank_cols(k, CH), T.ecol[:, 0:1], ALU.is_equal, banks=[k, k + 1])
+        else:
+            tk = act("oh%d" % j, [t_ne], cols(T.ab, a, b), bank_cols(k, CH), ACT.Abs, [k, k + 1], bias=T.nege[:, 0:1])
+            tk = act("oh%d" % j, [tk], cols(T.oh, a, b), cols(T.ab, a, b), ACT.Relu, bias=1.0, scale=-1.0)
+        mark("oh", 0, a, b, tk)
+
+    def kid_pieces():
+        k0, k1 = T.kidi[:, 0:192], T.kidi[:, 192:384]
+        l_k0, l_k1 = got["kid0"], got["kid1"]
+
+        def pc(i):
+            return T.pcs[:, 192 * i:192 * (i + 1)]
+        t_p1 = ts("p1", [l_k0], pc(1), k0, -8.0, ALU.add, 0.0, ALU.max)
+        t_ka = ts("ka", [l_k1], T.ka[:], k1, 2048.0, ALU.add)
+        t_kl = ts("kl", [l_k1], T.kl[:], k1, 63, ALU.bitwise_and)
+        t_p0 = tt("p0", [t_p1], pc(0), k0, pc(1), ALU.subtract)
+        t_kb = ts("ka", [t_ka], T.kb[:], T.ka[:], 6, ALU.logical_shift_right, 63, ALU.bitwise_and)
+        t_p2 = ts("kl", [t_kl], pc(2), T.kl[:], 8192.0, ALU.mult)
+        t_p3 = ts("ka", [t_kb], pc(3), T.kb[:], -32.0, ALU.add, 524288.0, ALU.mult)
+        got["pieces"] = (t_p0, t_p1, t_p2, t_p3)
+
+    def kid_rows():
+        for i, tk in enumerate(got["pieces"]):
+            tk = dma("y", "kt", [tk, t_k0], T.kt[i::16, :], T.pcs[:, 192 * i:192 * (i + 1)])
+        mark("kt", 0, 0, S, tk)
+
+    def node_list():
+        mark("nl", 0, 0, S, cp("nl", [got["nd0"]], T.nl0[:], T.ndi[:]))
+
+    def border_list():
+        mark("bd", 0, 0, BS, cp("bl", [got["bd"]], T.bdl[:], T.bdi[:]))
 
     calls = border_calls(rank, cores, topo)
     arrive = 0
-    for q in range(n):
+    for q in range(len(cores)):
         for c in border_calls(q, cores, topo):
-            for b, dst, engs in c:
+            for b, dst, engs, via in c:
                 if dst == rank:
-                    arrive += len(engs)
+                    arrive += len(engs if via is None else topo.engines(via, core))
     sent = [0]
 
     def B(name, d):
         return T["%s%d" % (name, d)]
 
-    pfree = {0: [t_oh[0]], 1: [t_oh[0]], 2: [t_oh[1]]}
-    kfree = {0: [t_oh[1]], 1: [t_ab], 2: [t_ab]}
-    st = {}
+    def e_vec(d, a, b):
+        mark("e", d, a, b, tt("e%d" % a, done("nl", d, a, b) + done("x", 0, a, b) + [got["hist"]], cols(B("e", d), a, b),
+                              T.hs[:].indirect(lst(B("nl", d), a, b)), cols(T.xs, a, b), ALU.subtract))
 
-    def g1_gather(d, j):
-        st["hn", j] = sg("hn%d" % j, [st["nl", j], l_h], ch(B("hn", d), j), T.hs[:], lc(B("nl", d), j))
+    def e_copy(d, a, b, e="y"):
+        deps, out, in_ = done("e", d, a, b), cols(B("ec", d), a, b), cols(B("e", d), a, b)
+        if e == "y":
+            tk = dma("y", "ecp%d" % a, deps, out, in_)
+        elif e == "g":
+            tk = op("g", "ecg%d" % a, deps, lambda: g.affine_select(out, in_, [[0, b - a]], ALU.is_ge, 0.0, 0, 0))
+        elif e == "v":
+            tk = cp("ecv%d" % a, deps, out, in_)
+        else:
+            tk = act("ecs%d" % a, deps, out, in_, ACT.Copy)
+        mark("ec", d, a, b, tk)
 
-    def g1_sub(d, j):
-        st["e", j] = tt("e%d" % j, [st["hn", j], l_x[j]], ch(B("e", d), j), ch(B("hn", d), j), ch(T.xs, j), ALU.subtract)
-        if j == 0 and d > 0:
-            st["ec"] = dma("y", "ecp", [st["e", 0]], B("ec", d)[:], ch(B("e", d), 0))
-        if j == 1 and d == 0:
-            st["ec"] = cp("ecv", [st["e", 0]], B("ec", d)[:], ch(B("e", d), 0))
+    def e_gather(d, a, b):
+        mark("hn", d, a, b, sg("hn%d" % a, done("nl", d, a, b) + [got["hist"]], cols(T.hn, a, b), T.hs[:], lst(B("nl", d), a, b)))
 
-    def g1_direct(d, j):
-        st["e", j] = tt("e%d" % j, [st["nl", j], l_h, l_x[j]], ch(B("e", d), j),
-                        T.hs[:].indirect(lc(B("nl", d), j)), ch(T.xs, j), ALU.subtract)
+    def e_sub(d, a, b):
+        mark("e", d, a, b, tt("e%d" % a, done("hn", d, a, b) + done("x", 0, a, b), cols(B("e", d), a, b),
+                              cols(T.hn, a, b), cols(T.xs, a, b), ALU.subtract))
 
-    def border(d, i):
-        c = calls[i]
-        b0, b1 = c[0][0], c[-1][0] + 1
-        tk = sg("bg%d" % i, [st["e", 0], st["e", 1], st["e", 2], t_bl], B("sb", d)[:, G * b0:G * b1],
-                B("e", d)[:, 0:S], T.bdl[:, 8 * b0:8 * b1])
+    def border(d, i, e):
+        a, b = G * calls[i][0][0], G * (calls[i][-1][0] + 1)
+        deps = done("e", d, 0, S) + done("bd", 0, 0, BS)
+        if e == "s":
+            tk = sg("bg%d" % i, deps, cols(B("sb", d), a, b), B("e", d)[:, 0:S], lst(T.bdl, a, b))
+        else:
+            tk = cp("bg%d" % i, deps, cols(B("sb", d), a, b), B("e", d)[:, 0:S].indirect(lst(T.bdl, a, b)))
+        mark("sb", d, i, i + 1, tk)
         need("g", [tk])
         trs = []
-        for b, dst, engs in c:
-            rid, pid, _se = topo.addr(cores[dst])
+        for b, dst, engs, via in calls[i]:
+            rid, pid, _se = topo.addr(cores[dst] if via is None else via)
             trs.append(RemoteDMATransfer(
                 dst_ids=[DstId(rid=rid, pnc=pid)], dma_engine_mask=bits(engs), remote_sem=T.sem["arr%d" % d],
-                src=B("sb", d)[:, G * b:G * (b + 1)], dst=B("e", d)[:, S + G * b:S + G * (b + 1)]))
+                src=B("sb", d)[:, G * b:G * (b + 1)],
+                dst=B("e", d)[:, S + G * b:S + G * (b + 1)] if via is None else B("sb", d)[:, 0:G]))
             sent[0] += len(engs)
         g.remote_dma_fused(trs, local_sem=T.sem.snd)
 
+    def hold_loads(name, a, b):
+        need("y", done(name, 0, a, b))
+
     def kid_gather(d, j):
-        st["kg", j] = sg("kg%d" % j, [st["nl", j]] + t_kt, ch(B("kg", d), j), T.kt[:], lc(B("nl", d), j))
+        a, b = KC[j], KC[j + 1]
+        mark("kg", d, a, b, sg("kg%d" % a, done("nl", d, a, b) + done("kt", 0, 0, S), cols(B("kg", d), a, b), T.kt[:],
+                               lst(B("nl", d), a, b)))
 
     def kid_sum(d, j):
-        st["k", j] = select("k%d" % j, [st["kg", j], t_z] + kfree[j], kbank(j), B("kg", d), j, d == DEP - 1)
+        a, b = KC[j], KC[j + 1]
+        mark("ks", d, a, b, select("k%d" % j, done("kg", d, a, b) + done("oh", 0, 0, S) + [t_z], "kid", B("kg", d), a, b, d == DEP - 1))
 
-    def way_pick(d, j):
-        if d == 0:
-            st["nbh", j] = ts("nbh%d" % j, [l_nb[j]], ch(T.nbh, j), ch(T.nbi, j), -2048.0, ALU.add)
-        st["q", j] = tt("q%d" % j, [st["nl", j], st["nbh", j]] + t_oh, ch(B("q", d), j),
-                        T.oh[:].indirect(lc(B("nl", d), j)), ch(T.nbh, j), ALU.mult)
+    def nb_half(j):
+        a, b = CH * j, CH * (j + 1)
+        mark("nbh", 0, a, b, ts("nbh%d" % j, done("nb", 0, a, b), cols(T.nbh, a, b), cols(T.nbi, a, b), -2048.0, ALU.add))
+
+    def t_gather(d, a, b):
+        mark("tq", d, a, b, sg("tq%d" % a, done("nl", d, a, b) + done("oh", 0, 0, S), cols(T.tq, a, b), T.oh[:], lst(B("nl", d), a, b)))
+
+    def pick(d, a, b, gathered=False):
+        if gathered:
+            deps, rows = done("tq", d, a, b), cols(T.tq, a, b)
+        else:
+            deps, rows = done("nl", d, a, b) + done("oh", 0, 0, S), T.oh[:].indirect(lst(B("nl", d), a, b))
+        mark("q", d, a, b, tt("q%d" % a, deps + done("nbh", 0, a, b), cols(B("q", d), a, b), rows, cols(T.nbh, a, b), ALU.mult))
 
     def p_sum(d, j):
-        st["p", j] = select("ps%d" % j, [st["q", j], t_z] + pfree[j], pbank(j), B("q", d), j, False)
+        a, b = PC[j], PC[j + 1]
+        mark("ps", d, a, b, select("ps%d" % j, done("q", d, a, b) + [t_z], "partner", B("q", d), a, b))
 
-    def p_list(d, j):
-        st["pl", j] = ts("pl%d" % j, [st["p", j]], lc(B("pl", d), j), pbank(j), 2048.0, ALU.add)
-        pfree[j] = [st["pl", j]]
+    def p_list(d, j, k=1):
+        a, b = PC[j], PC[j + k]
+        s, banks = sums("partner", a, b)
+        mark("pl", d, a, b, ts("pl%d" % j, done("ps", d, a, b), lst(B("pl", d), a, b), s, 2048.0, ALU.add, banks=banks))
 
-    def arr(d):
-        return ("arr%d" % d, arrive)
+    def window(d):
+        return done("e", d, 0, S) + [("arr%d" % d, arrive)]
 
-    def g3_direct(d, j):
-        st["cm", j] = tt("cm%d" % j, [st["pl", j], st["e", 0], st["e", 1], st["e", 2], st["ec"], arr(d)],
-                         ch(B("cm", d), j), B("e", d)[:].indirect(lc(B("pl", d), j)), B("ec", d)[:], ALU.is_gt)
+    def c_vec(d, a, b):
+        mark("cm", d, a, b, tt("cm%d" % a, done("pl", d, a, b) + done("ec", d, a, b) + window(d), cols(B("cm", d), a, b),
+                               B("e", d)[:].indirect(lst(B("pl", d), a, b)), cols(B("ec", d), a, b), ALU.is_gt))
 
-    def g3_gather(d, j):
-        st["ep", j] = sg("ep%d" % j, [st["pl", j], arr(d)], ch(B("ep", d), j - 1), B("e", d)[:], lc(B("pl", d), j))
+    def c_gather(d, a, b):
+        mark("ep", d, a, b, sg("ep%d" % a, done("pl", d, a, b) + window(d), cols(T.ep, a, b), B("e", d)[:], lst(B("pl", d), a, b)))
 
-    def g3_cmp(d, j):
-        st["cm", j] = tt("cm%d" % j, [st["ep", j]], ch(B("cm", d), j), ch(B("ep", d), j - 1), ch(B("e", d), j), ALU.is_gt)
+    def c_cmp(d, a, b):
+        mark("cm", d, a, b, tt("cm%d" % a, done("ep", d, a, b) + done("e", d, a, b), cols(B("cm", d), a, b),
+                               cols(T.ep, a, b), cols(B("e", d), a, b), ALU.is_gt))
 
     def c_sum(d, j):
-        st["c", j] = select("c%d" % j, [st["cm", j]], cbank(j), B("cm", d), j, d == DEP - 1)
+        a, b = KC[j], KC[j + 1]
+        mark("cnt", d, a, b, select("c%d" % j, done("cm", d, a, b), "count", B("cm", d), a, b, d == DEP - 1))
 
-    def step(d, j):
-        a = ts("sa%d" % j, [st["c", j], st["k", j]], lc(B("sf", d), j), cbank(j), 7.5, ALU.is_lt, 2.0 ** -13, ALU.max)
-        b = tt("sb%d" % j, [a], lc(B("ti", d), j), lc(B("sf", d), j), kbank(j), ALU.mult)
-        kfree[j] = [b]
-        c = ts("sc%d" % j, [b], lc(B("ui", d), j), lc(B("ti", d), j), 4095, ALU.bitwise_and)
-        if d < DEP - 1:
-            st["nl", j] = cp("sd%d" % j, [c], lc(B("nl", d + 1), j), lc(B("ui", d), j))
-        else:
-            f = cp("sd%d" % j, [c], lc(T.yf, j), lc(B("ui", d), j))
-            st["y", j] = dma("y", "y%d" % j, [f], ch(T.y, j), lc(T.yf, j))
+    def step(d, a, b):
+        (cnt, bc), (kid, bk) = sums("count", a, b), sums("kid", a, b)
+        r = {}
 
-    def middle(d):
-        border(d, 0)
-        border(d, 1)
-        if d == 0:
-            kid_gather(d, 0)
-        way_pick(d, 0)
-        kid_gather(d, 1)
-        kid_sum(d, 0)
-        p_sum(d, 0)
-        way_pick(d, 1)
-        p_list(d, 0)
-        kid_gather(d, 2)
-        p_sum(d, 1)
-        kid_sum(d, 1)
-        way_pick(d, 2)
-        p_list(d, 1)
-        p_sum(d, 2)
+        def s1():
+            r[1] = ts("sa%d" % a, done("cnt", d, a, b), lst(B("sf", d), a, b), cnt, 7.5, ALU.is_lt, 2.0 ** -13, ALU.max, banks=bc)
 
+        def s2():
+            r[2] = tt("sa%d" % a, [r[1]] + done("ks", d, a, b), lst(B("ti", d), a, b), lst(B("sf", d), a, b), kid, ALU.mult, banks=bk)
+
+        def s3():
+            r[3] = ts("sa%d" % a, [r[2]], lst(B("ui", d), a, b), lst(B("ti", d), a, b), 4095, ALU.bitwise_and)
+
+        def s4():
+            if d < DEP - 1:
+                mark("nl", d + 1, a, b, cp("sa%d" % a, [r[3]], lst(B("nl", d + 1), a, b), lst(B("ui", d), a, b)))
+            else:
+                f = cp("sa%d" % a, [r[3]], lst(T.yf, a, b), lst(B("ui", d), a, b))
+                dma("y", "y", [f], cols(T.y, a, b), lst(T.yf, a, b))
+        return [s1, s2, s3, s4]
+
+    def run(*chains):
+        for i in range(max(len(c) for c in chains)):
+            for c in chains:
+                if i < len(c):
+                    c[i]()
+
+    for name in ("way", "kid0", "nd0", "kid1", "hist", "bd"):
+        fetch(name)
+    load("x", T.xs, T.x, 0)
+    way_spread()
+    node_list()
+    way_onehot(2, "s")
+    border_list()
+    kid_pieces()
+    kid_rows()
+    load("x", T.xs, T.x, 1)
+    load("x", T.xs, T.x, 2)
     for j in range(3):
-        st["nl", j] = t_nl
-    g1_gather(0, 0)
-    g1_direct(0, 2)
-    g1_gather(0, 1)
-    g1_sub(0, 0)
-    g1_sub(0, 1)
-    middle(0)
-    for d in range(DEP):
-        more = d < DEP - 1
-        g3_direct(d, 0)
-        g3_gather(d, 1)
-        p_list(d, 2)
-        g3_gather(d, 2)
-        g3_cmp(d, 1)
-        c_sum(d, 0)
+        load("nb", T.nbi, T.nb, j)
+    way_onehot(0, "v")
+    e_vec(0, 0, 640)
+    way_onehot(1, "v")
+    e_vec(0, 1536, 2 * CH)
+    e_gather(0, CH, 1536)
+    e_gather(0, 640, CH)
+    e_gather(0, 2 * CH, S)
+    e_sub(0, CH, 1536)
+    e_sub(0, 640, CH)
+    e_sub(0, 2 * CH, S)
+    t_gather(0, 0, CH)
+    border(0, 0, "s")
+    border(0, 1, "s")
+    nb_half(0)
+    pick(0, 0, CH, True)
+    nb_half(1)
+    kid_gather(0, 0)
+    border(0, 2, "s")
+    e_copy(0, 0, CH, "g")
+    pick(0, CH, 2 * CH)
+    nb_half(2)
+    kid_gather(0, 1)
+    kid_gather(0, 2)
+    kid_sum(0, 0)
+    p_sum(0, 0)
+    p_sum(0, 1)
+    p_list(0, 0, 2)
+    pick(0, 2 * CH, S)
+    kid_sum(0, 1)
+    p_sum(0, 2)
+    for d in range(DEP - 1):
+        n = d + 1
+        c_gather(d, CH, 2 * CH)
+        c_vec(d, 0, CH)
         kid_sum(d, 2)
-        step(d, 0)
+        p_list(d, 2)
+        c_gather(d, 2 * CH, 2432)
+        c_sum(d, 0)
+        c_cmp(d, CH, 2 * CH)
+        c_cmp(d, 2 * CH, 2432)
+        run(step(d, 0, CH))
+        c_gather(d, 2432, S)
+        c_cmp(d, 2432, S)
+        e_gather(n, 0, HF)
+        e_vec(n, HF, CH)
         c_sum(d, 1)
-        g3_cmp(d, 2)
-        if more:
-            g1_gather(d + 1, 0)
-        step(d, 1)
+        e_sub(n, 0, HF)
+        e_copy(n, 0, CH, "y")
         c_sum(d, 2)
-        if more:
-            g1_gather(d + 1, 1)
-            g1_sub(d + 1, 0)
-        step(d, 2)
-        if more:
-            kid_gather(d + 1, 0)
-            g1_direct(d + 1, 2)
-            g1_sub(d + 1, 1)
-            middle(d + 1)
+        kid_gather(n, 0)
+        run(step(d, CH, S))
+        kid_sum(n, 0)
+        e_vec(n, 2 * CH, S)
+        e_gather(n, CH, 1536)
+        e_gather(n, 1536, 2 * CH)
+        t_gather(n, 640, CH)
+        e_sub(n, CH, 1536)
+        e_sub(n, 1536, 2 * CH)
+        for i in range(3):
+            border(n, i, "s")
+        pick(n, CH, 2 * CH)
+        p_sum(n, 1)
+        pick(n, 0, 640)
+        pick(n, 640, CH, True)
+        kid_gather(n, 1)
+        pick(n, 2176, S)
+        p_sum(n, 0)
+        kid_gather(n, 2)
+        p_list(n, 0, 2)
+        kid_sum(n, 1)
+        pick(n, 2 * CH, 2176)
+        p_sum(n, 2)
+    d = DEP - 1
+    s0, s1, s2 = step(d, 0, CH), step(d, CH, 2 * CH), step(d, 2 * CH, S)
+    c_vec(d, 0, CH)
+    kid_sum(d, 2)
+    c_gather(d, CH, 2 * CH)
+    p_list(d, 2)
+    c_gather(d, 2 * CH, 2560)
+    c_cmp(d, CH, 2 * CH)
+    c_sum(d, 0)
+    c_gather(d, 2560, 2944)
+    run(s0[:1])
+    c_cmp(d, 2 * CH, 2560)
+    c_cmp(d, 2560, 2944)
+    c_sum(d, 1)
+    c_gather(d, 2944, S)
+    run(s1[:1])
+    c_cmp(d, 2944, S)
+    c_sum(d, 2)
+    run(s0[1:3])
+    run(s1[1:3])
+    run(s0[3:])
+    run(s2[:1], s1[3:])
+    run(s2[1:])
 
     g.wait_ge(T.sem.snd, sent[0])
-    need("y", [st["y", j] for j in range(3)])
-    need("y", [(nm, c) for nm, c in count.items() if top.get(nm, 0) < c])
+    for nm, c in count.items():
+        if top.get(nm, 0) < c:
+            g.sync.wait_ge(T.sem[nm], c)

from concourse.bass import DstId, RemoteDMATransfer
from concourse.mybir import AluOpType as ALU, ActivationFunctionType as ACT

S = 3072
G = 128
NB = 7
BS = NB * G
BC = BS // 16
W = S + BS
DEP = 4
CH = 1024
NC = CH // 16
HF = 512
KC = (0, 1024, 2048, S)
PC = (0, 1024, 2048, S)

SCRATCH = {
    "ps": ("psum", [128, 4096], "float32"),
    "ones": ("sbuf", [128, 768], "bfloat16"),
    "bc": ("sbuf", [128, 768], "bfloat16"),
    "z": ("sbuf", [128, 144], "bfloat16"),
    "zt": ("sbuf", [128, 8], "bfloat16"),
    "pi": ("sbuf", [128, 8], "int32"),
    "pe": ("sbuf", [128, 8], "int32"),
    "ecol": ("sbuf", [128, 8], "float32"),
    "nege": ("sbuf", [128, 8], "float32"),
    "wayi": ("sbuf", [128, 512], "int32"),
    "wayb": ("sbuf", [128, 512], "bfloat16"),
    "kidi": ("sbuf", [128, 384], "int32"),
    "ka": ("sbuf", [128, 192], "int32"),
    "kb": ("sbuf", [128, 192], "int32"),
    "kl": ("sbuf", [128, 192], "int32"),
    "pcs": ("sbuf", [128, 768], "bfloat16"),
    "ndi": ("sbuf", [128, 192], "int32"),
    "bdi": ("sbuf", [128, BC], "int32"),
    "bdl": ("sbuf", [128, BC], "uint16"),
    "hs": ("sbuf", [128, S], "bfloat16"),
    "xs": ("sbuf", [128, S], "bfloat16"),
    "nbi": ("sbuf", [128, S], "int32"),
    "nbh": ("sbuf", [128, S], "float16"),
    "oh": ("sbuf", [128, S], "bfloat16"),
    "kt": ("sbuf", [128, S], "bfloat16"),
    "ab": ("sbuf", [128, S], "bfloat16"),
    "hn": ("sbuf", [128, S], "bfloat16"),
    "ep": ("sbuf", [128, S], "bfloat16"),
    "tq": ("sbuf", [128, S], "bfloat16"),
    "yf": ("sbuf", [128, 192], "float32"),
}
for _d in range(DEP):
    SCRATCH["e%d" % _d] = ("sbuf", [128, W], "bfloat16")
    SCRATCH["ec%d" % _d] = ("sbuf", [128, 2 * CH], "bfloat16")
    SCRATCH["q%d" % _d] = ("sbuf", [128, S], "float16")
    SCRATCH["kg%d" % _d] = ("sbuf", [128, S], "bfloat16")
    SCRATCH["cm%d" % _d] = ("sbuf", [128, S], "bfloat16")
    SCRATCH["sb%d" % _d] = ("sbuf", [128, BS], "bfloat16")
    SCRATCH["sf%d" % _d] = ("sbuf", [128, 192], "float32")
    SCRATCH["ti%d" % _d] = ("sbuf", [128, 192], "int32")
    SCRATCH["ui%d" % _d] = ("sbuf", [128, 192], "int32")
    SCRATCH["nl%d" % _d] = ("sbuf", [128, 192], "uint16")
    SCRATCH["pl%d" % _d] = ("sbuf", [128, 192], "uint16")

SEMAPHORES = ["snd"] + ["arr%d" % _d for _d in range(DEP)] + ["s%d" % _i for _i in range(140)]


def bits(engs):
    m = 0
    for e in engs:
        m |= 1 << e
    return m


def border_calls(q, cores, topo):
    n = len(cores)
    src = cores[q]
    dst = [(q + b + 1) % n for b in range(NB)]
    off = [b for b in range(NB) if topo.chip(cores[dst[b]]) != topo.chip(src)]
    oe = topo.engines(src, cores[dst[off[0]]])
    here = topo.chip(src)
    plane = [b for b in off if topo.same_plane(here, topo.chip(cores[dst[b]]))]
    mate = [b for b in off if topo.mates(here, topo.chip(cores[dst[b]]))]
    far = [b for b in off if b not in plane and b not in mate]
    helpers = [c for c in topo.cores_of(src) if c not in cores and topo.die(c) == topo.die(src)]
    free = [e for e in topo.engines(src, helpers[0]) if e not in oe]
    out = []
    for mine, engs in ((plane, oe + free), (far, oe), (mate, oe)):
        w = len(engs) // len(mine)
        out.append([(b, dst[b], engs[i * w:(i + 1) * w], helpers[i] if mine is plane else None) for i, b in enumerate(mine)])
    for b in range(NB):
        if b not in off:
            near = [c for c in out[1:] if c[0][0] == b + 1 or c[-1][0] == b - 1][0]
            near.append((b, dst[b], free[0::2], None))
            near.sort()
    return out


def hand_on(g, core, T, topo):
    cores = list(T.cores)
    for q in range(len(cores)):
        for b, dst, engs, via in border_calls(q, cores, topo)[0]:
            if via == core:
                rid, pid, _se = topo.addr(cores[dst])
                mine = topo.engines(core, cores[dst])
                for d in range(DEP):
                    g.wait_ge(T.sem["arr%d" % d], len(engs))
                    g.remote_dma(T["e%d" % d][:, S + G * b:S + G * (b + 1)], T["sb%d" % d][:, 0:G], T.sem["arr%d" % d],
                                 T.sem.snd, pid, rid, bits(mine))
                g.wait_ge(T.sem.snd, DEP * len(mine))


def rank_program(g, core, T, topo):
    rank = T.rank_of(core)
    if rank is None:
        hand_on(g, core, T, topo)
        return
    cores = list(T.cores)
    Q = {"g": g, "v": g.vector, "s": g.scalar, "t": g.tensor, "y": g.sync}
    V, A, P = g.vector, g.scalar, g.tensor
    names = {}
    count = {}
    seen = {k: {} for k in Q}
    top = {}
    before = {}
    bank_use = {b: {} for b in range(8)}
    made = {}

    def need(e, deps):
        for d in reversed(deps):
            nm, c = d
            if seen[e].get(nm, 0) < c:
                Q[e].wait_ge(T.sem[nm], c)
                seen[e][nm] = c
                top[nm] = max(top.get(nm, 0), c)
                for k, v in before.get(d, {}).items():
                    seen[e][k] = max(seen[e].get(k, 0), v)

    def need_banks(e, banks):
        for b in banks:
            need(e, [tk for q, tk in bank_use[b].items() if q != e])

    def op(e, role, deps, fn, inc=1, banks=()):
        need(e, deps)
        need_banks(e, banks)
        if role not in names:
            names[role] = "s%d" % len(names)
        nm = names[role]
        count[nm] = count.get(nm, 0) + inc
        fn().then_inc(T.sem[nm], inc)
        before[nm, count[nm]] = dict(seen[e])
        for b in banks:
            bank_use[b][e] = (nm, count[nm])
        return (nm, count[nm])

    def dma(e, role, deps, out, in_):
        return op(e, role, deps, lambda: Q[e].dma_start(out, in_), 16)

    def ts(role, deps, out, in0, s1, o0, s2=None, o1=None, banks=()):
        if o1 is None:
            return op("v", role, deps, lambda: V.tensor_scalar(out, in0, s1, None, o0), 1, banks)
        return op("v", role, deps, lambda: V.tensor_scalar(out, in0, s1, s2, o0, o1), 1, banks)

    def tt(role, deps, out, a, b, o, banks=()):
        return op("v", role, deps, lambda: V.tensor_tensor(out, a, b, o), 1, banks)

    def cp(role, deps, out, a):
        return op("v", role, deps, lambda: V.tensor_copy(out, a))

    def act(role, deps, out, a, func, banks=(), **kw):
        return op("s", role, deps, lambda: A.activation(out, a, func, **kw), 1, banks)

    def sg(role, deps, out, win, off):
        return act(role, deps, out, win.indirect(off), ACT.Copy)

    def mark(name, d, a, b, tk):
        made.setdefault((name, d), []).append((a, b, tk))

    def done(name, d, a, b):
        got = [m for m in made[name, d] if m[0] < b and a < m[1]]
        assert sum(min(m[1], b) - max(m[0], a) for m in got) == b - a
        return [m[2] for m in got]

    def cols(t, a, b):
        return t[:, a:b]

    def lst(t, a, b):
        return t[:, a // 16:b // 16]

    ps = T.ps

    def bank_cols(bank, k):
        return ps[:, HF * bank:HF * bank + k]

    def sums(kind, a, b):
        if kind == "partner":
            c = 6 * HF + (a - PC[2]) // 16
        else:
            c = {"kid": HF, "count": 3 * HF}[kind] + (a - KC[1]) // 16
        e = c + (b - a) // 16
        return ps[:, c:e], list(range(c // HF, (e - 1) // HF + 1))

    def select(role, deps, kind, src, a, b, rows=False):
        z = T.z
        out, banks = sums(kind, a, b)
        need("t", deps)
        need_banks("t", banks)

        def rhs(r):
            if rows:
                k = (b - a) // 16
                return src[:, a + k * r:a + k * (r + 1)]
            return src[:, a + r:b:16]
        for r in range(15):
            P.matmul(out, z[:, 15 - r:143 - r], rhs(r), r == 0, False)
        return op("t", role, [], lambda: P.matmul(out, z[:, 0:128], rhs(15), False, True), 1, banks)

    def load(name, out, in_, j):
        a, b = CH * j, CH * (j + 1)
        mark(name, 0, a, b, dma("y", "l_%s%d" % (name, j), [], cols(out, a, b), cols(in_, a, b)))

    whole = {"way": (T.wayi[0:48, :], T.way[:]), "kid0": (T.kidi[:, 0:192], T.kid0[:]), "kid1": (T.kidi[:, 192:384], T.kid1[:]),
             "nd0": (T.ndi[:], T.nd0[:]), "hist": (T.hs[:], T.hist[:]), "bd": (T.bdi[:], T.bd[:])}
    got = {}

    def fetch(name):
        got[name] = dma("s" if name in ("kid0", "kid1", "bd") else "y", "l_" + name, [], *whole[name])

    t_pi = op("g", "pi", [], lambda: g.iota(T.pi[:, 0:1], [[0, 1]], 0, 1))
    t_one = op("v", "one", [], lambda: V.memset(T.ones[:], 1.0))
    t_z0 = op("v", "z0", [], lambda: V.memset(T.z[:], 0.0))
    t_bc = op("g", "bc", [t_one], lambda: g.affine_select(
        T.bc[0:48, :], T.ones[0:48, :], [[-1, 6], [-6, 8], [0, 16]], ALU.is_equal, 0.0, 0, 1))
    t_zt = op("g", "zt", [], lambda: g.affine_select(T.zt[:], T.ones[:, 0:8], [[-16, 8]], ALU.is_ge, 0.0, 0, 1))
    t_z = op("g", "z", [t_zt, t_z0], lambda: g.affine_select(
        T.z[:, 15:143:16], T.zt[:], [[16, 8]], ALU.is_ge, 0.0, 15, -1))
    t_pe = ts("pe", [t_pi], T.pe[:, 0:1], T.pi[:, 0:1], 15, ALU.bitwise_and)
    t_k0 = op("v", "kz", [], lambda: V.memset(T.kt[:], 0.0))
    t_ec = cp("ec", [t_pe], T.ecol[:, 0:1], T.pe[:, 0:1])
    t_ne = ts("ne", [t_pe], T.nege[:, 0:1], T.pe[:, 0:1], -1.0, ALU.mult)

    wbank = {4: 2, 5: 3, 0: 6, 1: 7, 2: 4, 3: 5}

    def way_spread():
        t_wb = cp("wb", [got["way"]], T.wayb[0:48, :], T.wayi[0:48, :])
        for t, b in wbank.items():
            got["spread"] = op("t", "wm%d" % t, [t_wb, t_bc], lambda: P.matmul(
                bank_cols(b, HF), T.bc[0:48, 128 * t:128 * (t + 1)], T.wayb[0:48, :], True, True), 1, [b])

    def way_onehot(j, e):
        assert got["spread"]
        a, b, k = CH * j, CH * (j + 1), wbank[2 * j]
        if e == "v":
            tk = ts("oh%d" % j, [t_ec], cols(T.oh, a, b), bank_cols(k, CH), T.ecol[:, 0:1], ALU.is_equal, banks=[k, k + 1])
        else:
            tk = act("oh%d" % j, [t_ne], cols(T.ab, a, b), bank_cols(k, CH), ACT.Abs, [k, k + 1], bias=T.nege[:, 0:1])
            tk = act("oh%d" % j, [tk], cols(T.oh, a, b), cols(T.ab, a, b), ACT.Relu, bias=1.0, scale=-1.0)
        mark("oh", 0, a, b, tk)

    def kid_pieces():
        k0, k1 = T.kidi[:, 0:192], T.kidi[:, 192:384]
        l_k0, l_k1 = got["kid0"], got["kid1"]

        def pc(i):
            return T.pcs[:, 192 * i:192 * (i + 1)]
        t_p1 = ts("p1", [l_k0], pc(1), k0, -8.0, ALU.add, 0.0, ALU.max)
        t_ka = ts("ka", [l_k1], T.ka[:], k1, 2048.0, ALU.add)
        t_kl = ts("kl", [l_k1], T.kl[:], k1, 63, ALU.bitwise_and)
        t_p0 = tt("p0", [t_p1], pc(0), k0, pc(1), ALU.subtract)
        t_kb = ts("ka", [t_ka], T.kb[:], T.ka[:], 6, ALU.logical_shift_right, 63, ALU.bitwise_and)
        t_p2 = ts("kl", [t_kl], pc(2), T.kl[:], 8192.0, ALU.mult)
        t_p3 = ts("ka", [t_kb], pc(3), T.kb[:], -32.0, ALU.add, 524288.0, ALU.mult)
        got["pieces"] = (t_p0, t_p1, t_p2, t_p3)

    def kid_rows():
        for i, tk in enumerate(got["pieces"]):
            tk = dma("y", "kt", [tk, t_k0], T.kt[i::16, :], T.pcs[:, 192 * i:192 * (i + 1)])
        mark("kt", 0, 0, S, tk)

    def node_list():
        mark("nl", 0, 0, S, cp("nl", [got["nd0"]], T.nl0[:], T.ndi[:]))

    def border_list():
        mark("bd", 0, 0, BS, cp("bl", [got["bd"]], T.bdl[:], T.bdi[:]))

    calls = border_calls(rank, cores, topo)
    arrive = 0
    for q in range(len(cores)):
        for c in border_calls(q, cores, topo):
            for b, dst, engs, via in c:
                if dst == rank:
                    arrive += len(engs if via is None else topo.engines(via, core))
    sent = [0]

    def B(name, d):
        return T["%s%d" % (name, d)]

    def e_vec(d, a, b):
        mark("e", d, a, b, tt("e%d" % a, done("nl", d, a, b) + done("x", 0, a, b) + [got["hist"]], cols(B("e", d), a, b),
                              T.hs[:].indirect(lst(B("nl", d), a, b)), cols(T.xs, a, b), ALU.subtract))

    def e_copy(d, a, b, e="y"):
        deps, out, in_ = done("e", d, a, b), cols(B("ec", d), a, b), cols(B("e", d), a, b)
        if e == "y":
            tk = dma("y", "ecp%d" % a, deps, out, in_)
        elif e == "g":
            tk = op("g", "ecg%d" % a, deps, lambda: g.affine_select(out, in_, [[0, b - a]], ALU.is_ge, 0.0, 0, 0))
        elif e == "v":
            tk = cp("ecv%d" % a, deps, out, in_)
        else:
            tk = act("ecs%d" % a, deps, out, in_, ACT.Copy)
        mark("ec", d, a, b, tk)

    def e_gather(d, a, b):
        mark("hn", d, a, b, sg("hn%d" % a, done("nl", d, a, b) + [got["hist"]], cols(T.hn, a, b), T.hs[:], lst(B("nl", d), a, b)))

    def e_sub(d, a, b):
        mark("e", d, a, b, tt("e%d" % a, done("hn", d, a, b) + done("x", 0, a, b), cols(B("e", d), a, b),
                              cols(T.hn, a, b), cols(T.xs, a, b), ALU.subtract))

    def border(d, i, e):
        a, b = G * calls[i][0][0], G * (calls[i][-1][0] + 1)
        deps = done("e", d, 0, S) + done("bd", 0, 0, BS)
        if e == "s":
            tk = sg("bg%d" % i, deps, cols(B("sb", d), a, b), B("e", d)[:, 0:S], lst(T.bdl, a, b))
        else:
            tk = cp("bg%d" % i, deps, cols(B("sb", d), a, b), B("e", d)[:, 0:S].indirect(lst(T.bdl, a, b)))
        mark("sb", d, i, i + 1, tk)
        need("g", [tk])
        trs = []
        for b, dst, engs, via in calls[i]:
            rid, pid, _se = topo.addr(cores[dst] if via is None else via)
            trs.append(RemoteDMATransfer(
                dst_ids=[DstId(rid=rid, pnc=pid)], dma_engine_mask=bits(engs), remote_sem=T.sem["arr%d" % d],
                src=B("sb", d)[:, G * b:G * (b + 1)],
                dst=B("e", d)[:, S + G * b:S + G * (b + 1)] if via is None else B("sb", d)[:, 0:G]))
            sent[0] += len(engs)
        g.remote_dma_fused(trs, local_sem=T.sem.snd)

    def hold_loads(name, a, b):
        need("y", done(name, 0, a, b))

    def kid_gather(d, j):
        a, b = KC[j], KC[j + 1]
        mark("kg", d, a, b, sg("kg%d" % a, done("nl", d, a, b) + done("kt", 0, 0, S), cols(B("kg", d), a, b), T.kt[:],
                               lst(B("nl", d), a, b)))

    def kid_sum(d, j):
        a, b = KC[j], KC[j + 1]
        mark("ks", d, a, b, select("k%d" % j, done("kg", d, a, b) + done("oh", 0, 0, S) + [t_z], "kid", B("kg", d), a, b, d == DEP - 1))

    def nb_half(j):
        a, b = CH * j, CH * (j + 1)
        mark("nbh", 0, a, b, ts("nbh%d" % j, done("nb", 0, a, b), cols(T.nbh, a, b), cols(T.nbi, a, b), -2048.0, ALU.add))

    def t_gather(d, a, b):
        mark("tq", d, a, b, sg("tq%d" % a, done("nl", d, a, b) + done("oh", 0, 0, S), cols(T.tq, a, b), T.oh[:], lst(B("nl", d), a, b)))

    def pick(d, a, b, gathered=False):
        if gathered:
            deps, rows = done("tq", d, a, b), cols(T.tq, a, b)
        else:
            deps, rows = done("nl", d, a, b) + done("oh", 0, 0, S), T.oh[:].indirect(lst(B("nl", d), a, b))
        mark("q", d, a, b, tt("q%d" % a, deps + done("nbh", 0, a, b), cols(B("q", d), a, b), rows, cols(T.nbh, a, b), ALU.mult))

    def p_sum(d, j):
        a, b = PC[j], PC[j + 1]
        mark("ps", d, a, b, select("ps%d" % j, done("q", d, a, b) + [t_z], "partner", B("q", d), a, b))

    def p_list(d, j, k=1):
        a, b = PC[j], PC[j + k]
        s, banks = sums("partner", a, b)
        mark("pl", d, a, b, ts("pl%d" % j, done("ps", d, a, b), lst(B("pl", d), a, b), s, 2048.0, ALU.add, banks=banks))

    def window(d):
        return done("e", d, 0, S) + [("arr%d" % d, arrive)]

    def c_vec(d, a, b):
        mark("cm", d, a, b, tt("cm%d" % a, done("pl", d, a, b) + done("ec", d, a, b) + window(d), cols(B("cm", d), a, b),
                               B("e", d)[:].indirect(lst(B("pl", d), a, b)), cols(B("ec", d), a, b), ALU.is_gt))

    def c_gather(d, a, b):
        mark("ep", d, a, b, sg("ep%d" % a, done("pl", d, a, b) + window(d), cols(T.ep, a, b), B("e", d)[:], lst(B("pl", d), a, b)))

    def c_cmp(d, a, b):
        mark("cm", d, a, b, tt("cm%d" % a, done("ep", d, a, b) + done("e", d, a, b), cols(B("cm", d), a, b),
                               cols(T.ep, a, b), cols(B("e", d), a, b), ALU.is_gt))

    def c_sum(d, j):
        a, b = KC[j], KC[j + 1]
        mark("cnt", d, a, b, select("c%d" % j, done("cm", d, a, b), "count", B("cm", d), a, b, d == DEP - 1))

    def step(d, a, b):
        (cnt, bc), (kid, bk) = sums("count", a, b), sums("kid", a, b)
        r = {}

        def s1():
            r[1] = ts("sa%d" % a, done("cnt", d, a, b), lst(B("sf", d), a, b), cnt, 7.5, ALU.is_lt, 2.0 ** -13, ALU.max, banks=bc)

        def s2():
            r[2] = tt("sa%d" % a, [r[1]] + done("ks", d, a, b), lst(B("ti", d), a, b), lst(B("sf", d), a, b), kid, ALU.mult, banks=bk)

        def s3():
            r[3] = ts("sa%d" % a, [r[2]], lst(B("ui", d), a, b), lst(B("ti", d), a, b), 4095, ALU.bitwise_and)

        def s4():
            if d < DEP - 1:
                mark("nl", d + 1, a, b, cp("sa%d" % a, [r[3]], lst(B("nl", d + 1), a, b), lst(B("ui", d), a, b)))
            else:
                f = cp("sa%d" % a, [r[3]], lst(T.yf, a, b), lst(B("ui", d), a, b))
                dma("y", "y", [f], cols(T.y, a, b), lst(T.yf, a, b))
        return [s1, s2, s3, s4]

    def run(*chains):
        for i in range(max(len(c) for c in chains)):
            for c in chains:
                if i < len(c):
                    c[i]()

    for name in ("way", "kid0", "nd0", "kid1", "hist", "bd"):
        fetch(name)
    load("x", T.xs, T.x, 0)
    way_spread()
    node_list()
    way_onehot(2, "s")
    border_list()
    kid_pieces()
    kid_rows()
    load("x", T.xs, T.x, 1)
    load("x", T.xs, T.x, 2)
    for j in range(3):
        load("nb", T.nbi, T.nb, j)
    way_onehot(0, "v")
    e_vec(0, 0, 640)
    way_onehot(1, "v")
    e_vec(0, 1536, 2 * CH)
    e_gather(0, CH, 1536)
    e_gather(0, 640, CH)
    e_gather(0, 2 * CH, S)
    e_sub(0, CH, 1536)
    e_sub(0, 640, CH)
    e_sub(0, 2 * CH, S)
    t_gather(0, 0, CH)
    border(0, 0, "s")
    border(0, 1, "s")
    nb_half(0)
    pick(0, 0, CH, True)
    nb_half(1)
    kid_gather(0, 0)
    border(0, 2, "s")
    e_copy(0, 0, CH, "g")
    pick(0, CH, 2 * CH)
    nb_half(2)
    kid_gather(0, 1)
    kid_gather(0, 2)
    kid_sum(0, 0)
    p_sum(0, 0)
    p_sum(0, 1)
    p_list(0, 0, 2)
    pick(0, 2 * CH, S)
    kid_sum(0, 1)
    p_sum(0, 2)
    for d in range(DEP - 1):
        n = d + 1
        c_gather(d, CH, 2 * CH)
        c_vec(d, 0, CH)
        kid_sum(d, 2)
        p_list(d, 2)
        c_gather(d, 2 * CH, 2432)
        c_sum(d, 0)
        c_cmp(d, CH, 2 * CH)
        c_cmp(d, 2 * CH, 2432)
        run(step(d, 0, CH))
        c_gather(d, 2432, S)
        c_cmp(d, 2432, S)
        e_gather(n, 0, HF)
        e_vec(n, HF, CH)
        c_sum(d, 1)
        e_sub(n, 0, HF)
        e_copy(n, 0, CH, "y")
        c_sum(d, 2)
        kid_gather(n, 0)
        run(step(d, CH, S))
        kid_sum(n, 0)
        e_vec(n, 2 * CH, S)
        e_gather(n, CH, 1536)
        e_gather(n, 1536, 2 * CH)
        t_gather(n, 640, CH)
        e_sub(n, CH, 1536)
        e_sub(n, 1536, 2 * CH)
        for i in range(3):
            border(n, i, "s")
        pick(n, CH, 2 * CH)
        p_sum(n, 1)
        pick(n, 0, 640)
        pick(n, 640, CH, True)
        kid_gather(n, 1)
        pick(n, 2176, S)
        p_sum(n, 0)
        kid_gather(n, 2)
        p_list(n, 0, 2)
        kid_sum(n, 1)
        pick(n, 2 * CH, 2176)
        p_sum(n, 2)
    d = DEP - 1
    s0, s1, s2 = step(d, 0, CH), step(d, CH, 2 * CH), step(d, 2 * CH, S)
    c_vec(d, 0, CH)
    kid_sum(d, 2)
    c_gather(d, CH, 2 * CH)
    p_list(d, 2)
    c_gather(d, 2 * CH, 2560)
    c_cmp(d, CH, 2 * CH)
    c_sum(d, 0)
    c_gather(d, 2560, 2944)
    run(s0[:1])
    c_cmp(d, 2 * CH, 2560)
    c_cmp(d, 2560, 2944)
    c_sum(d, 1)
    c_gather(d, 2944, S)
    run(s1[:1])
    c_cmp(d, 2944, S)
    c_sum(d, 2)
    run(s0[1:3])
    run(s1[1:3])
    run(s0[3:])
    run(s2[:1], s1[3:])
    run(s2[1:])

    g.wait_ge(T.sem.snd, sent[0])
    for nm, c in count.items():
        if top.get(nm, 0) < c:
            g.sync.wait_ge(T.sem[nm], c)
